import numpy as np
import ml_dtypes


def mxq(x, axis, fmt="e4m3"):
    dtype, down = {"e4m3": (ml_dtypes.float8_e4m3fn, 7), "e5m2": (ml_dtypes.float8_e5m2, 14)}[fmt]
    v = np.moveaxis(np.asarray(x, np.float32).astype(ml_dtypes.bfloat16).astype(np.float64), axis, -1)
    blocks = v.reshape(v.shape[:-1] + (-1, 32))
    amax = np.abs(blocks).max(-1, keepdims=True)
    byte = np.maximum(np.where(amax > 0, np.frexp(amax)[1] - 1 + 127, 0) - down, 1)
    scale = np.exp2(byte - 127.0)
    codes = (blocks / scale).astype(np.float32).astype(dtype).astype(np.float64)
    return np.moveaxis((codes * scale).reshape(v.shape), -1, axis)


WIDE = False


def mx_kscale(k):
    if not WIDE:
        return np.ones(k)
    levels = np.array([10, -10, 5, -5, 0])
    if k % 512:
        return np.exp2(np.random.permutation(np.resize(levels, k // 32))).repeat(32)
    a = np.empty((k // 512, 16))
    for p in range(k // 512):
        a[p, :8] = np.random.permutation(np.resize(levels, 8))
        for g in range(8):
            far = levels[np.abs(levels - a[p, g]) >= 10]
            a[p, g + 8] = far[np.random.randint(len(far))]
    return np.exp2(a.ravel()).repeat(32)


BF16 = ml_dtypes.bfloat16


def bf(x):
    return np.asarray(x, np.float32).astype(BF16)


def f64(x):
    return np.asarray(x).astype(np.float64)

def planes(Y):
    n, m = Y.shape
    b = f64(bf(Y)).reshape(n // 32, 32, m)
    amax = np.abs(b).max(1)
    byte = np.clip(np.where(amax > 0, np.frexp(amax)[1] - 1 + 127 - 7, 1), 1, 254)
    codes = (b * np.exp2(127.0 - byte)[:, None, :]).reshape(n, m).astype(np.float32).astype(ml_dtypes.float8_e4m3fn).view(np.uint8)
    words = codes.reshape(n // 512, 128, 4, m).transpose(0, 1, 3, 2)
    return np.ascontiguousarray(words), np.ascontiguousarray(byte.astype(np.uint8).reshape(n // 512, 16, m))


B, N, C, M = 2, 1024, 512, 512


def softmax(v, axis):
    e = np.exp(v - v.max(axis=axis, keepdims=True))
    return e / e.sum(axis=axis, keepdims=True)


def setup_inputs():
    s, u = mx_kscale(N), mx_kscale(M)
    return {"fa": bf(np.random.standard_normal((B, N, C)) * 2.0 * s[None, :, None]),
            "lb": bf(np.random.standard_normal((B, N, M)) * 1.5),
            "lv": bf(np.random.standard_normal((B, N, M)) * 1.5),
            "t": bf(np.random.standard_normal(N) * np.sqrt(N) / 16.0 / s),
            "p": bf((1.0 + 0.1 * np.random.standard_normal(M)) * u),
            "r": bf(np.random.standard_normal(M) * np.sqrt(M / 32.0) / u)}


def gather_descriptors(fa, lb, t, p):
    sb = softmax(f64(lb), 1)
    sbg = sb * f64(t)[None, :, None]
    pooled = mxq(f64(fa), 1, "e4m3").transpose(0, 2, 1) @ mxq(sbg, 1, "e4m3")
    return f64(p)[None, None, :] * pooled


def distribute_descriptors(g, lv, r):
    sv = softmax(f64(lv), 2)
    svg = sv * f64(r)[None, None, :]
    return mxq(svg, 2, "e4m3") @ mxq(g, 2, "e4m3").transpose(0, 2, 1)


def core(fa, lb, lv, t, p, r):
    g = gather_descriptors(fa, lb, t, p)
    return distribute_descriptors(g, lv, r)


def reference(fa, lb, lv, t, p, r):
    R_out = core(fa, lb, lv, t, p, r)
    words, scales = planes(np.moveaxis(R_out, 2, 0).reshape(512, -1))
    return R_out, words, scales

@@ -1,0 +1,293 @@
+from contextlib import ExitStack
+
+import concourse.mybir as mybir
+from concourse.masks import make_identity
+
+B, N, C, M = 2, 1024, 512, 512
+FLOPS = 2 * B * N * C * M * 2
+
+F32 = mybir.dt.float32
+BF16 = mybir.dt.bfloat16
+U32 = mybir.dt.uint32
+I32 = mybir.dt.int32
+U8 = mybir.dt.uint8
+FP8X4 = mybir.dt.float8_e4m3fn_x4
+ALU = mybir.AluOpType
+ACT = mybir.ActivationFunctionType
+P = 128
+
+GP_FA = True
+BANKS = 6
+ORDER = """f01 xB00 iA00 iA03 xA00 wB00 iA01 iA02 xA03 f00 iA11 xA01 wA00 xB02 xB01 iA10 tB00 xA02 wA01 tA0p0 iA12 wA03 xB03 xA10 wA02 f11 tA0p1 xB11 xB12 iA13 xB10 xA13 f10 wB01 tB01 qF0 qA0 xA11 xA12 wB02 m01 m00 tB02 g01 g00 qB00 qG0 qB01 qB02 o00 wA12 p01 wB10 wA13 p00 wB11 p02 tA1p1 tB10 wA10 o01 wA11 tB11 tA1p0 wB03 tB03 o02 qF1 qA1 xB13 qB11 m11 qB03 m10 wB12 g11 o03 g10 tB12 qB10 p03 qG1 s00 wB13 o10 s01 s03 qB12 s02 o11 tB13 p10 qB13 s10 o12 p12 o13 p11 s12 p13 s11 s13""".split()
+ON_VECTOR = set("""O10ev0 O10evT1 O11ev1 O11evT0 O12ev1 O12evT1 O13ev1 O13evT0""".split())
+LOADS = """gains p lv00 lb00 lb01 fa0 lv01 lv02 lb10 lb11 lv03 lv10 fa1 lv11 lv12 lv13""".split()
+
+
+def tile_doubleattentiongatherdistributesignedgai_x1_kernel(tc, fa, lb, lv, t, p, r, out_0, out_1, out_2):
+    nc = tc.nc
+    with ExitStack() as ctx:
+        keep = ctx.enter_context(tc.tile_pool(name="keep", bufs=1))
+        work = ctx.enter_context(tc.tile_pool(name="work", bufs=3))
+        gains = ctx.enter_context(tc.psum_pool(name="gains", bufs=1))
+        psum = ctx.enter_context(tc.psum_pool(name="psum", bufs=BANKS))
+        ctx.enter_context(tc.manual_schedule())
+
+        def kept(name, shape, dtype):
+            return keep.tile(shape, dtype, name=name, align_bytes=64)
+
+        def bank(shape, dtype):
+            return psum.tile(shape, dtype, name="bank")
+
+        def copy_out(name, out, in_):
+            if name in ON_VECTOR:
+                nc.vector.tensor_copy(out=out, in_=in_)
+            else:
+                nc.scalar.copy(out=out, in_=in_)
+
+        raw = {}
+        t_sb = kept("t_sb", [P, 2, 4], BF16)
+        r_sb = kept("r_sb", [P, 4], BF16)
+        p_sb = kept("p_sb", [P, 4], BF16)
+        for name in LOADS:
+            if name == "gains":
+                nc.scalar.dma_start(out=r_sb[:], in_=r.rearrange("(q j) -> q j", j=4))
+                nc.scalar.dma_start(out=t_sb[:], in_=t.rearrange("(g q j) -> q g j", g=2, j=4))
+                continue
+            if name == "p":
+                nc.scalar.dma_start(out=p_sb[:], in_=p.rearrange("(q j) -> q j", j=4))
+                continue
+            b = int(name[2])
+            if name[:2] == "lv":
+                h = int(name[3])
+                raw[name] = kept(name, [P, 2, M], BF16)
+                nc.sync.dma_start(out=raw[name][:], in_=lv[b, 256 * h : 256 * (h + 1), :].rearrange("(q j) m -> q j m", j=2))
+            elif name[:2] == "lb":
+                half = int(name[3])
+                raw[name] = kept(name, [P, 2, 4, 256], BF16)
+                for g in range(2):
+                    nc.sync.dma_start(
+                        out=raw[name][:, g],
+                        in_=lb[b, 512 * g : 512 * (g + 1), 256 * half : 256 * (half + 1)].rearrange("(q j) m -> q j m", j=4),
+                    )
+            else:
+                raw[name] = kept(name, [P, 2, 4 * C], BF16)
+                nc.sync.dma_start(out=raw[name][:], in_=fa[b].rearrange("(g q j) c -> q g (j c)", g=2, j=4))
+
+        ident32 = kept("ident32", [P, P], F32)
+        make_identity(nc, ident32[:])
+        ident16 = kept("ident16", [P, P], BF16)
+        make_identity(nc, ident16[:])
+
+        warm = kept("warm", [P, 2], F32)
+        nc.vector.memset(warm[:, 0:1], 0.0)
+        nc.scalar.activation(out=warm[:, 1:2], in_=warm[:, 0:1], func=ACT.Exp)
+
+        r_bank = gains.tile([P, 2, P], F32, name="r_bank")
+        t_bank = gains.tile([P, 4, P], F32, name="t_bank")
+        r_words = r_sb[:].bitcast(F32)
+        for u in range(2):
+            nc.tensor.transpose(r_bank[:, u, :], r_words[:, u : u + 1].to_broadcast([P, P]), ident32[:])
+        t_words = t_sb[:].rearrange("q g j -> q (g j)").bitcast(F32)
+        for k in range(4):
+            nc.tensor.transpose(t_bank[:, k, :], t_words[:, k : k + 1].to_broadcast([P, P]), ident32[:])
+        r_gain = r_bank[:].rearrange("p u q -> p (u q)").bitcast(BF16)
+        t_gain = t_bank[:].rearrange("p k q -> p (k q)").bitcast(BF16)
+
+        tiles = {}
+        fa_g = [kept("fa_g%s" % (b,), [P, 2, C, 4], BF16) for b in range(B)]
+        sb_g = [kept("sb_g%s" % (b,), [P, 2, M * 4], BF16) for b in range(B)]
+        g_g = [kept("g_g%s" % (b,), [P, C * 4], BF16) for b in range(B)]
+        fa_codes = [kept("fa_codes%s" % (b,), [P, 2, C], U32) for b in range(B)]
+        fa_scales = [kept("fa_scales%s" % (b,), [P, 2, C], U8) for b in range(B)]
+        sb_codes = [kept("sb_codes%s" % (b,), [P, 2, M], U32) for b in range(B)]
+        sb_scales = [kept("sb_scales%s" % (b,), [P, 2, M], U8) for b in range(B)]
+        g_codes = [kept("g_codes%s" % (b,), [P, C], U32) for b in range(B)]
+        g_scales = [kept("g_scales%s" % (b,), [P, C], U8) for b in range(B)]
+        out_scales = [kept("out_scales%s" % (k,), [P, 512], U8) for k in range(4)]
+        words_hbm = out_1[0].rearrange("p m t -> p (m t)").bitcast(I32)
+        scales_hbm = out_2[0].bitcast(I32)
+
+        def quantize(codes, scales, in_):
+            nc.vector.quantize_mx(out=codes.bitcast(FP8X4), scales=scales, in_=in_)
+
+        def interleave_fa(b, g):
+            src = raw["fa%s" % (b,)][:, g, :].rearrange("q (j c) -> q c j", j=4)
+            for s in range(4 if GP_FA else 2):
+                w = C // (4 if GP_FA else 2)
+                cols = slice(s * w, (s + 1) * w)
+                if GP_FA:
+                    nc.gpsimd.tensor_scalar(out=fa_g[b][:, g, cols, :], in0=src[:, cols, :], scalar1=1.0, scalar2=1.0, op0=ALU.mult, op1=ALU.mult)
+                else:
+                    copy_out("F%si%s%s" % (b, g, s,), fa_g[b][:, g, cols, :], src[:, cols, :])
+
+        def turn_in(unit):
+            b, a = int(unit[1]), int(unit[2])
+            turned = bank([P, 8, P], BF16)
+            src = raw["lb%s%s" % (b, a // 2,)]
+            for g in range(2):
+                for j in range(4):
+                    nc.tensor.transpose(turned[:, 4 * g + j, :], src[:, g, j, P * (a % 2) : P * (a % 2 + 1)], ident16[:])
+            tiles["in", unit] = turned
+
+        def exps(unit):
+            rows = 1 if unit[0] == "A" else 2
+            width = 1024 // rows
+            neg = work.tile([P, rows, width], BF16, name="neg")
+            top = kept("top%s" % (unit,), [P, rows], F32)
+            total = kept("total%s" % (unit,), [P, rows], F32)
+            e = work.tile([P, rows, width], F32, name="e", bufs=10)
+            for j in range(rows):
+                if unit[0] == "A":
+                    src = tiles["in", unit][:].rearrange("p s q -> p (s q)")
+                else:
+                    src = raw["lv" + unit[1:]][:, j, :]
+                nc.vector.tensor_scalar(out=neg[:, j, :], in0=src, scalar1=-1.0, scalar2=None, op0=ALU.mult, op1=ALU.min, accum_out=top[:, j : j + 1])
+            for j in range(rows):
+                if unit[0] == "A":
+                    src = neg[:, j, :].rearrange("p (k e q) -> p k q e", k=4, e=2)
+                    dst = e[:, j, :].rearrange("p (k q e) -> p k q e", k=4, e=2)
+                else:
+                    src = neg[:, j, :].rearrange("p (q u e) -> p u q e", u=2, e=2)
+                    dst = e[:, j, :].rearrange("p (u q e) -> p u q e", u=2, e=2)
+                nc.scalar.activation(out=dst, in_=src, func=ACT.Exp, scale=-1.0, bias=top[:, j : j + 1], accum_out=total[:, j : j + 1])
+            tiles["e", unit] = e
+            tiles["total", unit] = total
+
+        def invert(unit):
+            total = tiles["total", unit]
+            inv = kept("inv%s" % (unit,), list(total.shape), F32)
+            nc.vector.reciprocal(out=inv[:], in_=total[:])
+            tiles["inv", unit] = inv
+
+        def weigh(unit, j):
+            rows = 1 if unit[0] == "A" else 2
+            if j == 0:
+                tiles["w", unit] = work.tile([P, rows, 1024 // rows], BF16, name="w", bufs=5)
+            nc.vector.scalar_tensor_tensor(
+                out=tiles["w", unit][:, j, :], in0=tiles["e", unit][:, j, :], scalar=tiles["inv", unit][:, j : j + 1],
+                in1=t_gain if unit[0] == "A" else r_gain, op0=ALU.mult, op1=ALU.mult,
+            )
+
+        def turn_back(unit):
+            b = int(unit[1])
+            if unit[0] == "A":
+                pair = int(unit[3])
+                turned = []
+                for g in range(2):
+                    bk = bank([P, 2, 2 * P], F32)
+                    for a2 in range(2):
+                        words = tiles["w", "A%s%s" % (b, 2 * pair + a2,)][:, 0, :].bitcast(F32)
+                        for u in range(2):
+                            k = 2 * g + u
+                            nc.tensor.transpose(bk[:, u, P * a2 : P * (a2 + 1)], words[:, P * k : P * (k + 1)], ident32[:])
+                    turned.append(bk)
+                for g in range(2):
+                    dst = sb_g[b][:, g, :].bitcast(F32).rearrange("q (s i u) -> q s i u", s=4, u=2)
+                    copy_out("%sg%sev" % (unit, g,), dst[:, :, 64 * pair : 64 * (pair + 1), :], turned[g][:].rearrange("q u (i s) -> q s i u", s=4))
+            else:
+                bk = bank([P, 2, 2, P], F32)
+                for j in range(2):
+                    words = tiles["w", unit][:, j, :].bitcast(F32)
+                    for u in range(2):
+                        nc.tensor.transpose(bk[:, j, u, :], words[:, P * u : P * (u + 1)], ident32[:])
+                grouped = work.tile([P, 1024], BF16, name="sv_g", align_bytes=64, bufs=4)
+                copy_out("%sev" % (unit,), grouped[:].bitcast(F32).rearrange("q (k s) -> q k s", s=4), bk[:].rearrange("q j u k -> q k (j u)"))
+                tiles["sv_g", unit] = grouped
+
+        def quant_steps(unit):
+            b = int(unit[1])
+            if unit[0] == "A":
+                return [lambda g=g: quantize(sb_codes[b][:, g, :], sb_scales[b][:, g, :], sb_g[b][:, g, :]) for g in range(2)]
+            if unit[0] == "F":
+                return [lambda g=g: quantize(fa_codes[b][:, g, :], fa_scales[b][:, g, :], fa_g[b][:, g].rearrange("q c j -> q (c j)")) for g in range(2)]
+            if unit[0] == "G":
+                return [lambda: quantize(g_codes[b][:], g_scales[b][:], g_g[b][:])]
+            codes = kept("sv_codes%s" % (unit,), [P, 256], U32)
+            scales = kept("sv_scales%s" % (unit,), [P, 256], U8)
+            tiles["sv", unit[1:]] = (codes, scales)
+            return [lambda: quantize(codes[:], scales[:], tiles["sv_g", unit][:])]
+
+        def pool_maps(b, cc):
+            bk = bank([P, 4, P], F32)
+            cols = slice(P * cc, P * (cc + 1))
+            for s in range(4):
+                maps = slice(P * s, P * (s + 1))
+                for g in range(2):
+                    nc.tensor.matmul_mx(
+                        out=bk[:, s, :], lhsT=sb_codes[b][:, g, maps].bitcast(FP8X4), lhsT_scale=sb_scales[b][:, g, maps],
+                        rhs=fa_codes[b][:, g, cols].bitcast(FP8X4), rhs_scale=fa_scales[b][:, g, cols], start=(g == 0), stop=(g == 1),
+                    )
+            tiles["pooled", b, cc] = bk
+
+        def scale_pooled(b, cc):
+            dst = g_g[b][:].rearrange("p (s i j) -> p s i j", s=4, j=4)[:, :, 32 * cc : 32 * (cc + 1), :]
+            src = tiles["pooled", b, cc][:].rearrange("p j (i s) -> p s i j", s=4)
+            gain = p_sb[:].unsqueeze(1).unsqueeze(1).to_broadcast([P, 4, 32, 4])
+            nc.vector.tensor_tensor(out=dst, in0=src, in1=gain, op=ALU.mult)
+
+        def rows_out(unit):
+            b, h = int(unit[0]), int(unit[1])
+            codes, scales = tiles["sv", unit]
+            res = work.tile([P, 2, C], F32, name="res")
+            banks = []
+            for i in range(2):
+                bk = bank([P, C], F32)
+                cols = slice(P * i, P * (i + 1))
+                nc.tensor.matmul_mx(out=bk[:], lhsT=codes[:, cols].bitcast(FP8X4), lhsT_scale=scales[:, cols],
+                                    rhs=g_codes[b][:].bitcast(FP8X4), rhs_scale=g_scales[b][:], start=True, stop=True)
+                banks.append(bk)
+            for i in range(2):
+                copy_out("O%sev%s" % (unit, i,), res[:, i, :].rearrange("p (k s) -> p k s", s=4), banks[i][:].rearrange("p (s k) -> p k s", s=4))
+            nc.sync.dma_start(out=out_0[b, 256 * h : 256 * (h + 1), :].rearrange("(i p) c -> p i c", i=2), in_=res[:])
+
+        def planes_out(unit):
+            b = int(unit[0])
+            codes, scales = tiles["sv", unit]
+            grouped = work.tile([P, 2, P, 4], BF16, name="out_g", align_bytes=64, bufs=5)
+            banks = []
+            for i in range(2):
+                bk = bank([P, 4, P], F32)
+                cols = slice(P * i, P * (i + 1))
+                for s in range(4):
+                    chans = slice(P * s, P * (s + 1))
+                    nc.tensor.matmul_mx(out=bk[:, s, :], lhsT=g_codes[b][:, chans].bitcast(FP8X4), lhsT_scale=g_scales[b][:, chans],
+                                        rhs=codes[:, cols].bitcast(FP8X4), rhs_scale=scales[:, cols], start=True, stop=True)
+                banks.append(bk)
+            for i in range(2):
+                copy_out("O%sevT%s" % (unit, i,), grouped[:, i], banks[i][:].rearrange("p s k -> p k s"))
+            tiles["out_g", unit] = grouped
+
+        def planes_quant(unit):
+            k = 4 * int(unit[0]) + int(unit[1])
+            codes = work.tile([P, 256], U32, name="out_codes", align_bytes=64)
+            plane = out_scales[k // 2]
+            quantize(codes[:], plane[:, 256 * (k % 2) : 256 * (k % 2 + 1)], tiles["out_g", unit][:].rearrange("p i k s -> p (i k s)"))
+            nc.sync.dma_start(out=words_hbm[:, 256 * k : 256 * (k + 1)], in_=codes[:].bitcast(I32))
+            tiles["stored", k] = True
+            if ("stored", k ^ 1) in tiles:
+                for q in range(4):
+                    nc.sync.dma_start(out=scales_hbm[4 * q : 4 * q + 4, 128 * (k // 2) : 128 * (k // 2 + 1)],
+                                      in_=plane[32 * q : 32 * q + 4, :].bitcast(I32))
+
+        calls = []
+        last_vector = 0
+        for tok in ORDER:
+            kind, unit = tok[0], tok[1:]
+            if kind == "w":
+                calls = calls[:last_vector] + [(invert, (unit,))] + calls[last_vector:]
+                steps = [(weigh, (unit, j)) for j in range(1 if unit[0] == "A" else 2)]
+            elif kind == "q":
+                steps = [(lambda f: f(), (f,)) for f in quant_steps(unit)]
+            elif kind == "g":
+                steps = [(scale_pooled, (int(unit[0]), 2 * int(unit[1]) + k)) for k in range(2)]
+            elif kind == "m":
+                steps = [(pool_maps, (int(unit[0]), 2 * int(unit[1]) + k)) for k in range(2)]
+            elif kind == "f":
+                steps = [(interleave_fa, (int(unit[0]), int(unit[1])))]
+            else:
+                steps = [({"i": turn_in, "x": exps, "t": turn_back, "o": rows_out, "p": planes_out, "s": planes_quant}[kind], (unit,))]
+            calls.extend(steps)
+            if kind in "wqgxs":
+                last_vector = len(calls) - 1
+        for fn, args in calls:
+            fn(*args)

@@ -14,280 +14,303 @@ U8 = mybir.dt.uint8
 FP8X4 = mybir.dt.float8_e4m3fn_x4
 ALU = mybir.AluOpType
 ACT = mybir.ActivationFunctionType
-P = 128
 
-GP_FA = True
-BANKS = 6
-ORDER = """f01 xB00 iA00 iA03 xA00 wB00 iA01 iA02 xA03 f00 iA11 xA01 wA00 xB02 xB01 iA10 tB00 xA02 wA01 tA0p0 iA12 wA03 xB03 xA10 wA02 f11 tA0p1 xB11 xB12 iA13 xB10 xA13 f10 wB01 tB01 qF0 qA0 xA11 xA12 wB02 m01 m00 tB02 g01 g00 qB00 qG0 qB01 qB02 o00 wA12 p01 wB10 wA13 p00 wB11 p02 tA1p1 tB10 wA10 o01 wA11 tB11 tA1p0 wB03 tB03 o02 qF1 qA1 xB13 qB11 m11 qB03 m10 wB12 g11 o03 g10 tB12 qB10 p03 qG1 s00 wB13 o10 s01 s03 qB12 s02 o11 tB13 p10 qB13 s10 o12 p12 o13 p11 s12 p13 s11 s13""".split()
-ON_VECTOR = set("""O10ev0 O10evT1 O11ev1 O11evT0 O12ev1 O12evT1 O13ev1 O13evT0""".split())
-LOADS = """gains p lv00 lb00 lb01 fa0 lv01 lv02 lb10 lb11 lv03 lv10 fa1 lv11 lv12 lv13""".split()
+P = 128
+PACK = 4
+PASSES = N // (P * PACK)
+GROUP = 2 * P
+GROUPS = N // GROUP
+HALF = M // 2
+
+NEG_BUFS, EXP_BUFS, WEIGHTED_BUFS, SV_BUFS, COLS_BUFS = 4, 7, 8, 6, 4
+ROWS_BUFS, CODES_BUFS = 6, 8
+ROTATING_BANKS = 7
+
+LOADS = "lv00 lv01 lv02 lv03 lb00 lv10 lb01 lv13 lv11 lv12 lb10 fa0 lb11 fa1".split()
+
+ORDER = """
+turn:lb00 exp:lv00 turn:lb01 turn:lb02 turn:lb03 exp:lv01 exp:lv02 invert:lv00 exp:lv03 weigh:lv00 invert:lv01
+exp:lv10 exp:lb00 weigh:lv01 exp:lb01 turn:lb10 invert:lv03 exp:lb02 weigh:lv03 invert:lv10 turn:lb11 turn:lb12
+exp:lb03 lay:fa000 invert:lb00 weigh:lv10 weigh:lb00 lay:fa001 invert:lb01 lay:fa011 weigh:lb01 lay:fa010
+weigh:lb02 back:lb00 weigh:lb03 back:lb01 back:lv00 invert:lv02 exp:lb12 exp:lv11 quant:fa0 quant:sb0 turn:lb13
+exp:lb13 back:lv03 weigh:lv02 pool:00 pool:01 exp:lb10 invert:lv11 exp:lb11 gain:00 invert:lb11 back:lv10
+gain:01 back:lv02 lay:fa111 back:lv01 quant:lv00 quant:lv03 quant:g0 invert:lb10 cols:03 weigh:lb12 weigh:lb13
+weigh:lb11 weigh:lb10 rows:00 rows:03 back:lb11 quant:lv01 back:lb10 lay:fa101 quant:lv02 rows:02 lay:fa100
+lay:fa110 quant:fa1 quant:sb1 rows:01 exp:lv12 exp:lv13 cols:00 cols:01 weigh:lv11 pool:10 invert:lv12 gain:10
+pool:11 weigh:lv12 gain:11 quant:lv10 quant:g1 back:lv11 quant:lv11 store:00 store:03 invert:lv13 store:01
+back:lv12 cols:02 store:02 rows:10 quant:lv12 weigh:lv13 rows:11 cols:10 rows:12 back:lv13 quant:lv13 cols:11
+store:10 cols:12 store:11 store:12 rows:13 cols:13 store:13
+""".split()
+
+ON_VECTOR = set("cols:10:0 cols:12:0 cols:13:0 lay:fa100:0 lay:fa101:0 lay:fa110:0 rows:11:1 rows:12:0 rows:13:0".split())
 
 
 def tile_doubleattentiongatherdistributesignedgai_x1_kernel(tc, fa, lb, lv, t, p, r, out_0, out_1, out_2):
     nc = tc.nc
     with ExitStack() as ctx:
         keep = ctx.enter_context(tc.tile_pool(name="keep", bufs=1))
-        work = ctx.enter_context(tc.tile_pool(name="work", bufs=3))
-        gains = ctx.enter_context(tc.psum_pool(name="gains", bufs=1))
-        psum = ctx.enter_context(tc.psum_pool(name="psum", bufs=BANKS))
+        work = ctx.enter_context(tc.tile_pool(name="work", bufs=1))
+        fixed_psum = ctx.enter_context(tc.psum_pool(name="fixed_psum", bufs=1))
+        psum = ctx.enter_context(tc.psum_pool(name="psum", bufs=ROTATING_BANKS))
         ctx.enter_context(tc.manual_schedule())
 
         def kept(name, shape, dtype):
             return keep.tile(shape, dtype, name=name, align_bytes=64)
 
+        def rotating(name, bufs, shape, dtype):
+            return work.tile(shape, dtype, name=name, bufs=bufs, align_bytes=64)
+
         def bank(shape, dtype):
             return psum.tile(shape, dtype, name="bank")
 
-        def copy_out(name, out, in_):
-            if name in ON_VECTOR:
+        def copy(step, number, out, in_):
+            if "%s:%d" % (step, number) in ON_VECTOR:
                 nc.vector.tensor_copy(out=out, in_=in_)
             else:
                 nc.scalar.copy(out=out, in_=in_)
 
-        raw = {}
-        t_sb = kept("t_sb", [P, 2, 4], BF16)
-        r_sb = kept("r_sb", [P, 4], BF16)
-        p_sb = kept("p_sb", [P, 4], BF16)
-        for name in LOADS:
-            if name == "gains":
-                nc.scalar.dma_start(out=r_sb[:], in_=r.rearrange("(q j) -> q j", j=4))
-                nc.scalar.dma_start(out=t_sb[:], in_=t.rearrange("(g q j) -> q g j", g=2, j=4))
-                continue
-            if name == "p":
-                nc.scalar.dma_start(out=p_sb[:], in_=p.rearrange("(q j) -> q j", j=4))
-                continue
-            b = int(name[2])
-            if name[:2] == "lv":
-                h = int(name[3])
-                raw[name] = kept(name, [P, 2, M], BF16)
-                nc.sync.dma_start(out=raw[name][:], in_=lv[b, 256 * h : 256 * (h + 1), :].rearrange("(q j) m -> q j m", j=2))
-            elif name[:2] == "lb":
-                half = int(name[3])
-                raw[name] = kept(name, [P, 2, 4, 256], BF16)
-                for g in range(2):
-                    nc.sync.dma_start(
-                        out=raw[name][:, g],
-                        in_=lb[b, 512 * g : 512 * (g + 1), 256 * half : 256 * (half + 1)].rearrange("(q j) m -> q j m", j=4),
-                    )
-            else:
-                raw[name] = kept(name, [P, 2, 4 * C], BF16)
-                nc.sync.dma_start(out=raw[name][:], in_=fa[b].rearrange("(g q j) c -> q g (j c)", g=2, j=4))
-
-        ident32 = kept("ident32", [P, P], F32)
-        make_identity(nc, ident32[:])
-        ident16 = kept("ident16", [P, P], BF16)
-        make_identity(nc, ident16[:])
-
-        warm = kept("warm", [P, 2], F32)
-        nc.vector.memset(warm[:, 0:1], 0.0)
-        nc.scalar.activation(out=warm[:, 1:2], in_=warm[:, 0:1], func=ACT.Exp)
-
-        r_bank = gains.tile([P, 2, P], F32, name="r_bank")
-        t_bank = gains.tile([P, 4, P], F32, name="t_bank")
-        r_words = r_sb[:].bitcast(F32)
-        for u in range(2):
-            nc.tensor.transpose(r_bank[:, u, :], r_words[:, u : u + 1].to_broadcast([P, P]), ident32[:])
-        t_words = t_sb[:].rearrange("q g j -> q (g j)").bitcast(F32)
-        for k in range(4):
-            nc.tensor.transpose(t_bank[:, k, :], t_words[:, k : k + 1].to_broadcast([P, P]), ident32[:])
-        r_gain = r_bank[:].rearrange("p u q -> p (u q)").bitcast(BF16)
-        t_gain = t_bank[:].rearrange("p k q -> p (k q)").bitcast(BF16)
-
-        tiles = {}
-        fa_g = [kept("fa_g%s" % (b,), [P, 2, C, 4], BF16) for b in range(B)]
-        sb_g = [kept("sb_g%s" % (b,), [P, 2, M * 4], BF16) for b in range(B)]
-        g_g = [kept("g_g%s" % (b,), [P, C * 4], BF16) for b in range(B)]
-        fa_codes = [kept("fa_codes%s" % (b,), [P, 2, C], U32) for b in range(B)]
-        fa_scales = [kept("fa_scales%s" % (b,), [P, 2, C], U8) for b in range(B)]
-        sb_codes = [kept("sb_codes%s" % (b,), [P, 2, M], U32) for b in range(B)]
-        sb_scales = [kept("sb_scales%s" % (b,), [P, 2, M], U8) for b in range(B)]
-        g_codes = [kept("g_codes%s" % (b,), [P, C], U32) for b in range(B)]
-        g_scales = [kept("g_scales%s" % (b,), [P, C], U8) for b in range(B)]
-        out_scales = [kept("out_scales%s" % (k,), [P, 512], U8) for k in range(4)]
-        words_hbm = out_1[0].rearrange("p m t -> p (m t)").bitcast(I32)
-        scales_hbm = out_2[0].bitcast(I32)
-
         def quantize(codes, scales, in_):
             nc.vector.quantize_mx(out=codes.bitcast(FP8X4), scales=scales, in_=in_)
 
-        def interleave_fa(b, g):
-            src = raw["fa%s" % (b,)][:, g, :].rearrange("q (j c) -> q c j", j=4)
-            for s in range(4 if GP_FA else 2):
-                w = C // (4 if GP_FA else 2)
-                cols = slice(s * w, (s + 1) * w)
-                if GP_FA:
-                    nc.gpsimd.tensor_scalar(out=fa_g[b][:, g, cols, :], in0=src[:, cols, :], scalar1=1.0, scalar2=1.0, op0=ALU.mult, op1=ALU.mult)
-                else:
-                    copy_out("F%si%s%s" % (b, g, s,), fa_g[b][:, g, cols, :], src[:, cols, :])
-
-        def turn_in(unit):
-            b, a = int(unit[1]), int(unit[2])
-            turned = bank([P, 8, P], BF16)
-            src = raw["lb%s%s" % (b, a // 2,)]
-            for g in range(2):
-                for j in range(4):
-                    nc.tensor.transpose(turned[:, 4 * g + j, :], src[:, g, j, P * (a % 2) : P * (a % 2 + 1)], ident16[:])
-            tiles["in", unit] = turned
-
-        def exps(unit):
-            rows = 1 if unit[0] == "A" else 2
-            width = 1024 // rows
-            neg = work.tile([P, rows, width], BF16, name="neg")
-            top = kept("top%s" % (unit,), [P, rows], F32)
-            total = kept("total%s" % (unit,), [P, rows], F32)
-            e = work.tile([P, rows, width], F32, name="e", bufs=10)
-            for j in range(rows):
-                if unit[0] == "A":
-                    src = tiles["in", unit][:].rearrange("p s q -> p (s q)")
-                else:
-                    src = raw["lv" + unit[1:]][:, j, :]
-                nc.vector.tensor_scalar(out=neg[:, j, :], in0=src, scalar1=-1.0, scalar2=None, op0=ALU.mult, op1=ALU.min, accum_out=top[:, j : j + 1])
-            for j in range(rows):
-                if unit[0] == "A":
-                    src = neg[:, j, :].rearrange("p (k e q) -> p k q e", k=4, e=2)
-                    dst = e[:, j, :].rearrange("p (k q e) -> p k q e", k=4, e=2)
-                else:
-                    src = neg[:, j, :].rearrange("p (q u e) -> p u q e", u=2, e=2)
-                    dst = e[:, j, :].rearrange("p (u q e) -> p u q e", u=2, e=2)
-                nc.scalar.activation(out=dst, in_=src, func=ACT.Exp, scale=-1.0, bias=top[:, j : j + 1], accum_out=total[:, j : j + 1])
-            tiles["e", unit] = e
-            tiles["total", unit] = total
-
-        def invert(unit):
-            total = tiles["total", unit]
-            inv = kept("inv%s" % (unit,), list(total.shape), F32)
-            nc.vector.reciprocal(out=inv[:], in_=total[:])
-            tiles["inv", unit] = inv
-
-        def weigh(unit, j):
-            rows = 1 if unit[0] == "A" else 2
-            if j == 0:
-                tiles["w", unit] = work.tile([P, rows, 1024 // rows], BF16, name="w", bufs=5)
-            nc.vector.scalar_tensor_tensor(
-                out=tiles["w", unit][:, j, :], in0=tiles["e", unit][:, j, :], scalar=tiles["inv", unit][:, j : j + 1],
-                in1=t_gain if unit[0] == "A" else r_gain, op0=ALU.mult, op1=ALU.mult,
+        def matmul_mx(out, stationary, moving, start, stop):
+            nc.tensor.matmul_mx(
+                out=out, lhsT=stationary[0].bitcast(FP8X4), lhsT_scale=stationary[1],
+                rhs=moving[0].bitcast(FP8X4), rhs_scale=moving[1], start=start, stop=stop,
             )
 
-        def turn_back(unit):
-            b = int(unit[1])
-            if unit[0] == "A":
-                pair = int(unit[3])
-                turned = []
-                for g in range(2):
-                    bk = bank([P, 2, 2 * P], F32)
-                    for a2 in range(2):
-                        words = tiles["w", "A%s%s" % (b, 2 * pair + a2,)][:, 0, :].bitcast(F32)
-                        for u in range(2):
-                            k = 2 * g + u
-                            nc.tensor.transpose(bk[:, u, P * a2 : P * (a2 + 1)], words[:, P * k : P * (k + 1)], ident32[:])
-                    turned.append(bk)
-                for g in range(2):
-                    dst = sb_g[b][:, g, :].bitcast(F32).rearrange("q (s i u) -> q s i u", s=4, u=2)
-                    copy_out("%sg%sev" % (unit, g,), dst[:, :, 64 * pair : 64 * (pair + 1), :], turned[g][:].rearrange("q u (i s) -> q s i u", s=4))
+        r_sb = kept("r_sb", [P, PACK], BF16)
+        t_sb = kept("t_sb", [P, PASSES, PACK], BF16)
+        p_sb = kept("p_sb", [P, PACK], BF16)
+        nc.scalar.dma_start(out=r_sb[:], in_=r.rearrange("(q j) -> q j", j=PACK))
+        nc.scalar.dma_start(out=t_sb[:], in_=t.rearrange("(g q j) -> q g j", g=PASSES, j=PACK))
+        nc.scalar.dma_start(out=p_sb[:], in_=p.rearrange("(q j) -> q j", j=PACK))
+
+        raw = {}
+        for name in LOADS:
+            b = int(name[2])
+            if name.startswith("lv"):
+                first = GROUP * int(name[3])
+                raw[name] = kept(name, [P, 2, M], BF16)
+                nc.sync.dma_start(out=raw[name][:], in_=lv[b, first : first + GROUP, :].rearrange("(q s) m -> q s m", s=2))
+            elif name.startswith("lb"):
+                first = HALF * int(name[3])
+                raw[name] = kept(name, [P, PASSES, PACK, HALF], BF16)
+                for g in range(PASSES):
+                    rows = lb[b, P * PACK * g : P * PACK * (g + 1), first : first + HALF]
+                    nc.sync.dma_start(out=raw[name][:, g], in_=rows.rearrange("(q j) m -> q j m", j=PACK))
             else:
-                bk = bank([P, 2, 2, P], F32)
-                for j in range(2):
-                    words = tiles["w", unit][:, j, :].bitcast(F32)
+                raw[name] = kept(name, [P, PASSES, PACK * C], BF16)
+                nc.sync.dma_start(out=raw[name][:], in_=fa[b].rearrange("(g q j) c -> q g (j c)", g=PASSES, j=PACK))
+
+        ident32 = kept("ident32", [P, P], F32)
+        make_identity(nc, ident32[:])
+        zeros = kept("zeros", [P, P], F32)
+        nc.vector.memset(zeros[:], 0.0)
+        ones = kept("ones", [P, P], BF16)
+        nc.scalar.activation(out=ones[:], in_=zeros[:], func=ACT.Exp)
+        ident16 = kept("ident16", [P, P], BF16)
+        nc.gpsimd.affine_select(
+            out=ident16[:], in_=ones[:], compare_op=ALU.is_equal, fill=0.0, base=0, pattern=[[-1, P]], channel_multiplier=1
+        )
+
+        r_bank = fixed_psum.tile([P, 2, P], F32, name="r_bank")
+        t_bank = bank([P, 2 * PASSES, P], F32)
+        for gain_bank, gain_sb in ((r_bank, r_sb[:]), (t_bank, t_sb[:].rearrange("q g j -> q (g j)"))):
+            words = gain_sb.bitcast(F32)
+            for k in range(words.shape[1]):
+                nc.tensor.transpose(gain_bank[:, k, :], words[:, k : k + 1].to_broadcast([P, P]), ident32[:])
+        gain_row = {
+            "lv": r_bank[:].rearrange("p u q -> p (u q)").bitcast(BF16),
+            "lb": t_bank[:].rearrange("p k q -> p (k q)").bitcast(BF16),
+        }
+
+        operand = {}
+        for b in range(B):
+            for name, passes in (("fa%d" % b, PASSES), ("sb%d" % b, PASSES), ("g%d" % b, 1)):
+                operand[name] = (
+                    kept(name + "_bf16", [P, passes, C * PACK], BF16),
+                    kept(name + "_codes", [P, passes, C], U32),
+                    kept(name + "_scales", [P, passes, C], U8),
+                )
+        out_scales = [kept("out_scales%d" % b, [P, N], U8) for b in range(B)]
+        words_hbm = out_1[0].rearrange("p m j -> p (m j)").bitcast(I32)
+        scales_hbm = out_2[0].bitcast(I32)
+
+        made = {}
+        stored = []
+
+        def columns(name, g, first, width):
+            bf16, codes, scales = operand[name]
+            return codes[:, g, first : first + width], scales[:, g, first : first + width]
+
+        def sums_of(unit):
+            owner = unit if unit.startswith("lv") else unit[:3] + str(int(unit[3]) // 2)
+            if ("sums", owner) not in made:
+                made["sums", owner] = kept("sums_" + owner, [P, 2], F32)
+            return owner
+
+        def lay(unit):
+            name, g, first = unit[:3], int(unit[3]), HALF * int(unit[4])
+            src = raw[name][:, g, :].rearrange("q (j c) -> q j c", j=PACK)[:, :, first : first + HALF]
+            dst = operand[name][0][:, g, PACK * first : PACK * (first + HALF)]
+            copy("lay:" + unit, 0, dst.rearrange("q (c i j) -> q c j i", i=4, j=PACK), src.rearrange("q j (c i) -> q c j i", i=4))
+
+        def turn(unit):
+            a = int(unit[3])
+            src = raw[unit[:3] + str(a // 2)]
+            turned = bank([P, PASSES * PACK, P], BF16)
+            for g in range(PASSES):
+                for j in range(PACK):
+                    nc.tensor.transpose(turned[:, PACK * g + j, :], src[:, g, j, P * (a % 2) : P * (a % 2 + 1)], ident16[:])
+            made["turned", unit] = turned
+
+        def exp(unit):
+            of_lb = unit.startswith("lb")
+            rows = 1 if of_lb else 2
+            width = N // rows
+            neg = rotating("neg", NEG_BUFS, [P, rows, width], BF16)
+            neg_max = kept("neg_max_" + unit, [P, rows], F32)
+            sums = made["sums", sums_of(unit)]
+            values = rotating("values", EXP_BUFS, [P, rows, width], F32)
+            for s in range(rows):
+                src = made["turned", unit][:].rearrange("p k q -> p (k q)") if of_lb else raw[unit][:, s, :]
+                nc.vector.tensor_scalar(
+                    out=neg[:, s, :], in0=src, scalar1=-1.0, scalar2=None, op0=ALU.mult, op1=ALU.min, accum_out=neg_max[:, s : s + 1]
+                )
+            for s in range(rows):
+                src = neg[:, s, :].rearrange("p (k e q) -> p k q e" if of_lb else "p (q k e) -> p k q e", q=P, e=2)
+                column = int(unit[3]) % 2 if of_lb else s
+                nc.scalar.activation(
+                    out=values[:, s, :].rearrange("p (k q e) -> p k q e", q=P, e=2), in_=src, func=ACT.Exp, scale=-1.0,
+                    bias=neg_max[:, s : s + 1], accum_out=sums[:, column : column + 1],
+                )
+            made["values", unit] = values
+
+        def invert(unit):
+            made["inverse", unit] = kept("inverse_" + unit, [P, 2], F32)
+            nc.vector.reciprocal(out=made["inverse", unit][:], in_=made["sums", unit][:])
+
+        def weigh(unit):
+            values = made["values", unit]
+            rows = values.shape[1]
+            inverse = made["inverse", sums_of(unit)]
+            weighted = rotating("weighted", WEIGHTED_BUFS, list(values.shape), BF16)
+            for s in range(rows):
+                column = int(unit[3]) % 2 if rows == 1 else s
+                nc.vector.scalar_tensor_tensor(
+                    out=weighted[:, s, :], in0=values[:, s, :], scalar=inverse[:, column : column + 1],
+                    in1=gain_row[unit[:2]], op0=ALU.mult, op1=ALU.mult,
+                )
+            made["weighted", unit] = weighted
+
+        def back_lb(unit):
+            pair = int(unit[3])
+            banks = []
+            for g in range(PASSES):
+                banks.append(bank([P, 2, 2 * P], F32))
+                for a in range(2):
+                    words = made["weighted", unit[:3] + str(2 * pair + a)][:, 0, :].bitcast(F32)
                     for u in range(2):
-                        nc.tensor.transpose(bk[:, j, u, :], words[:, P * u : P * (u + 1)], ident32[:])
-                grouped = work.tile([P, 1024], BF16, name="sv_g", align_bytes=64, bufs=4)
-                copy_out("%sev" % (unit,), grouped[:].bitcast(F32).rearrange("q (k s) -> q k s", s=4), bk[:].rearrange("q j u k -> q k (j u)"))
-                tiles["sv_g", unit] = grouped
+                        k = 2 * g + u
+                        nc.tensor.transpose(banks[g][:, u, P * a : P * (a + 1)], words[:, P * k : P * (k + 1)], ident32[:])
+            share = HALF // PACK
+            for g in range(PASSES):
+                dst = operand["sb" + unit[2]][0][:, g, :].bitcast(F32).rearrange("q (s i u) -> q s i u", s=PACK, u=2)
+                src = banks[g][:].rearrange("q u (i s) -> q s i u", s=PACK)
+                copy("back:" + unit, g, dst[:, :, share * pair : share * (pair + 1), :], src)
 
-        def quant_steps(unit):
-            b = int(unit[1])
-            if unit[0] == "A":
-                return [lambda g=g: quantize(sb_codes[b][:, g, :], sb_scales[b][:, g, :], sb_g[b][:, g, :]) for g in range(2)]
-            if unit[0] == "F":
-                return [lambda g=g: quantize(fa_codes[b][:, g, :], fa_scales[b][:, g, :], fa_g[b][:, g].rearrange("q c j -> q (c j)")) for g in range(2)]
-            if unit[0] == "G":
-                return [lambda: quantize(g_codes[b][:], g_scales[b][:], g_g[b][:])]
-            codes = kept("sv_codes%s" % (unit,), [P, 256], U32)
-            scales = kept("sv_scales%s" % (unit,), [P, 256], U8)
-            tiles["sv", unit[1:]] = (codes, scales)
-            return [lambda: quantize(codes[:], scales[:], tiles["sv_g", unit][:])]
+        def back_lv(unit):
+            turned = bank([P, 2, 2, P], F32)
+            for s in range(2):
+                words = made["weighted", unit][:, s, :].bitcast(F32)
+                for u in range(2):
+                    nc.tensor.transpose(turned[:, s, u, :], words[:, P * u : P * (u + 1)], ident32[:])
+            sv = rotating("sv", SV_BUFS, [P, GROUP * PACK], BF16)
+            dst = sv[:].bitcast(F32).rearrange("q (k w) -> q k w", k=P)
+            copy("back:" + unit, 0, dst, turned[:].rearrange("q s u k -> q k (s u)"))
+            made["sv", unit] = sv
 
-        def pool_maps(b, cc):
-            bk = bank([P, 4, P], F32)
-            cols = slice(P * cc, P * (cc + 1))
-            for s in range(4):
-                maps = slice(P * s, P * (s + 1))
-                for g in range(2):
-                    nc.tensor.matmul_mx(
-                        out=bk[:, s, :], lhsT=sb_codes[b][:, g, maps].bitcast(FP8X4), lhsT_scale=sb_scales[b][:, g, maps],
-                        rhs=fa_codes[b][:, g, cols].bitcast(FP8X4), rhs_scale=fa_scales[b][:, g, cols], start=(g == 0), stop=(g == 1),
-                    )
-            tiles["pooled", b, cc] = bk
-
-        def scale_pooled(b, cc):
-            dst = g_g[b][:].rearrange("p (s i j) -> p s i j", s=4, j=4)[:, :, 32 * cc : 32 * (cc + 1), :]
-            src = tiles["pooled", b, cc][:].rearrange("p j (i s) -> p s i j", s=4)
-            gain = p_sb[:].unsqueeze(1).unsqueeze(1).to_broadcast([P, 4, 32, 4])
-            nc.vector.tensor_tensor(out=dst, in0=src, in1=gain, op=ALU.mult)
-
-        def rows_out(unit):
-            b, h = int(unit[0]), int(unit[1])
-            codes, scales = tiles["sv", unit]
-            res = work.tile([P, 2, C], F32, name="res")
-            banks = []
-            for i in range(2):
-                bk = bank([P, C], F32)
-                cols = slice(P * i, P * (i + 1))
-                nc.tensor.matmul_mx(out=bk[:], lhsT=codes[:, cols].bitcast(FP8X4), lhsT_scale=scales[:, cols],
-                                    rhs=g_codes[b][:].bitcast(FP8X4), rhs_scale=g_scales[b][:], start=True, stop=True)
-                banks.append(bk)
-            for i in range(2):
-                copy_out("O%sev%s" % (unit, i,), res[:, i, :].rearrange("p (k s) -> p k s", s=4), banks[i][:].rearrange("p (s k) -> p k s", s=4))
-            nc.sync.dma_start(out=out_0[b, 256 * h : 256 * (h + 1), :].rearrange("(i p) c -> p i c", i=2), in_=res[:])
-
-        def planes_out(unit):
-            b = int(unit[0])
-            codes, scales = tiles["sv", unit]
-            grouped = work.tile([P, 2, P, 4], BF16, name="out_g", align_bytes=64, bufs=5)
-            banks = []
-            for i in range(2):
-                bk = bank([P, 4, P], F32)
-                cols = slice(P * i, P * (i + 1))
-                for s in range(4):
-                    chans = slice(P * s, P * (s + 1))
-                    nc.tensor.matmul_mx(out=bk[:, s, :], lhsT=g_codes[b][:, chans].bitcast(FP8X4), lhsT_scale=g_scales[b][:, chans],
-                                        rhs=codes[:, cols].bitcast(FP8X4), rhs_scale=scales[:, cols], start=True, stop=True)
-                banks.append(bk)
-            for i in range(2):
-                copy_out("O%sevT%s" % (unit, i,), grouped[:, i], banks[i][:].rearrange("p s k -> p k s"))
-            tiles["out_g", unit] = grouped
-
-        def planes_quant(unit):
-            k = 4 * int(unit[0]) + int(unit[1])
-            codes = work.tile([P, 256], U32, name="out_codes", align_bytes=64)
-            plane = out_scales[k // 2]
-            quantize(codes[:], plane[:, 256 * (k % 2) : 256 * (k % 2 + 1)], tiles["out_g", unit][:].rearrange("p i k s -> p (i k s)"))
-            nc.sync.dma_start(out=words_hbm[:, 256 * k : 256 * (k + 1)], in_=codes[:].bitcast(I32))
-            tiles["stored", k] = True
-            if ("stored", k ^ 1) in tiles:
-                for q in range(4):
-                    nc.sync.dma_start(out=scales_hbm[4 * q : 4 * q + 4, 128 * (k // 2) : 128 * (k // 2 + 1)],
-                                      in_=plane[32 * q : 32 * q + 4, :].bitcast(I32))
-
-        calls = []
-        last_vector = 0
-        for tok in ORDER:
-            kind, unit = tok[0], tok[1:]
-            if kind == "w":
-                calls = calls[:last_vector] + [(invert, (unit,))] + calls[last_vector:]
-                steps = [(weigh, (unit, j)) for j in range(1 if unit[0] == "A" else 2)]
-            elif kind == "q":
-                steps = [(lambda f: f(), (f,)) for f in quant_steps(unit)]
-            elif kind == "g":
-                steps = [(scale_pooled, (int(unit[0]), 2 * int(unit[1]) + k)) for k in range(2)]
-            elif kind == "m":
-                steps = [(pool_maps, (int(unit[0]), 2 * int(unit[1]) + k)) for k in range(2)]
-            elif kind == "f":
-                steps = [(interleave_fa, (int(unit[0]), int(unit[1])))]
+        def back(unit):
+            if unit.startswith("lb"):
+                back_lb(unit)
             else:
-                steps = [({"i": turn_in, "x": exps, "t": turn_back, "o": rows_out, "p": planes_out, "s": planes_quant}[kind], (unit,))]
-            calls.extend(steps)
-            if kind in "wqgxs":
-                last_vector = len(calls) - 1
-        for fn, args in calls:
-            fn(*args)
+                back_lv(unit)
+
+        def quant(unit):
+            if unit.startswith("lv"):
+                codes = kept("sv_codes_" + unit, [P, GROUP], U32)
+                scales = kept("sv_scales_" + unit, [P, GROUP], U8)
+                quantize(codes[:], scales[:], made["sv", unit][:])
+                made["sv_mx", unit[2:]] = [(codes[:, P * i : P * (i + 1)], scales[:, P * i : P * (i + 1)]) for i in range(2)]
+            else:
+                bf16, codes, scales = operand[unit]
+                for g in range(bf16.shape[1]):
+                    quantize(codes[:, g, :], scales[:, g, :], bf16[:, g, :])
+
+        def pool(unit):
+            for chunk in (2 * int(unit[1]), 2 * int(unit[1]) + 1):
+                pooled = bank([P, PACK, P], F32)
+                for s in range(PACK):
+                    for g in range(PASSES):
+                        matmul_mx(
+                            pooled[:, s, :], columns("sb" + unit[0], g, P * s, P), columns("fa" + unit[0], g, P * chunk, P),
+                            start=(g == 0), stop=(g == PASSES - 1),
+                        )
+                made["pooled", unit[0], chunk] = pooled
+
+        def gain(unit):
+            share = P // PACK
+            for chunk in (2 * int(unit[1]), 2 * int(unit[1]) + 1):
+                dst = operand["g" + unit[0]][0][:, 0, :].rearrange("q (s i j) -> q s i j", s=PACK, j=PACK)
+                nc.vector.tensor_tensor(
+                    out=dst[:, :, share * chunk : share * (chunk + 1), :],
+                    in0=made["pooled", unit[0], chunk][:].rearrange("q j (i s) -> q s i j", s=PACK),
+                    in1=p_sb[:].unsqueeze(1).unsqueeze(1).to_broadcast([P, PACK, share, PACK]),
+                    op=ALU.mult,
+                )
+
+        def rows(unit):
+            b, first = int(unit[0]), GROUP * int(unit[1])
+            result = rotating("result", ROWS_BUFS, [P, 2, C], F32)
+            banks = []
+            for i in range(2):
+                banks.append(bank([P, C], F32))
+                matmul_mx(banks[i][:], made["sv_mx", unit][i], columns("g" + unit[0], 0, 0, C), start=True, stop=True)
+            for i in range(2):
+                dst = result[:, i, :].rearrange("p (k s) -> p k s", s=PACK)
+                copy("rows:" + unit, i, dst, banks[i][:].rearrange("p (s k) -> p k s", s=PACK))
+            nc.sync.dma_start(out=out_0[b, first : first + GROUP, :].rearrange("(i p) c -> p i c", i=2), in_=result[:])
+
+        def cols(unit):
+            result_bf16 = rotating("result_bf16", COLS_BUFS, [P, 2, P, PACK], BF16)
+            banks = []
+            for i in range(2):
+                banks.append(bank([P, PACK, P], F32))
+                for s in range(PACK):
+                    matmul_mx(banks[i][:, s, :], columns("g" + unit[0], 0, P * s, P), made["sv_mx", unit][i], start=True, stop=True)
+            for i in range(2):
+                copy("cols:" + unit, i, result_bf16[:, i], banks[i][:].rearrange("q s k -> q k s"))
+            made["result_bf16", unit] = result_bf16
+
+        def store(unit):
+            b, first = int(unit[0]), GROUP * int(unit[1])
+            codes = rotating("out_codes", CODES_BUFS, [P, GROUP], U32)
+            src = made["result_bf16", unit][:].rearrange("q i k s -> q (i k s)")
+            quantize(codes[:], out_scales[b][:, first : first + GROUP], src)
+            nc.sync.dma_start(out=words_hbm[:, N * b + first : N * b + first + GROUP], in_=codes[:].bitcast(I32))
+            stored.append(unit)
+            if len([done for done in stored if done[0] == unit[0]]) == GROUPS:
+                for quadrant in range(4):
+                    queue = nc.scalar if len(stored) == B * GROUPS and quadrant >= 2 else nc.sync
+                    queue.dma_start(
+                        out=scales_hbm[4 * quadrant : 4 * quadrant + 4, N // 4 * b : N // 4 * (b + 1)],
+                        in_=out_scales[b][32 * quadrant : 32 * quadrant + 4, :].bitcast(I32),
+                    )
+
+        steps = {
+            "lay": lay, "turn": turn, "exp": exp, "invert": invert, "weigh": weigh, "back": back, "quant": quant,
+            "pool": pool, "gain": gain, "rows": rows, "cols": cols, "store": store,
+        }
+        for step in ORDER:
+            name, unit = step.split(":")
+            steps[name](unit)

from contextlib import ExitStack

import concourse.mybir as mybir
from concourse.masks import make_identity

B, N, C, M = 2, 1024, 512, 512
FLOPS = 2 * B * N * C * M * 2

F32 = mybir.dt.float32
BF16 = mybir.dt.bfloat16
U32 = mybir.dt.uint32
I32 = mybir.dt.int32
U8 = mybir.dt.uint8
FP8X4 = mybir.dt.float8_e4m3fn_x4
ALU = mybir.AluOpType
ACT = mybir.ActivationFunctionType

P = 128
PACK = 4
PASSES = N // (P * PACK)
GROUP = 2 * P
GROUPS = N // GROUP
HALF = M // 2

NEG_BUFS, EXP_BUFS, WEIGHTED_BUFS, SV_BUFS, COLS_BUFS = 4, 7, 8, 6, 4
ROWS_BUFS, CODES_BUFS = 6, 8
ROTATING_BANKS = 7

LOADS = "lv00 lv01 lv02 lv03 lb00 lv10 lb01 lv13 lv11 lv12 lb10 fa0 lb11 fa1".split()

ORDER = """
turn:lb00 exp:lv00 turn:lb01 turn:lb02 turn:lb03 exp:lv01 exp:lv02 invert:lv00 exp:lv03 weigh:lv00 invert:lv01
exp:lv10 exp:lb00 weigh:lv01 exp:lb01 turn:lb10 invert:lv03 exp:lb02 weigh:lv03 invert:lv10 turn:lb11 turn:lb12
exp:lb03 lay:fa000 invert:lb00 weigh:lv10 weigh:lb00 lay:fa001 invert:lb01 lay:fa011 weigh:lb01 lay:fa010
weigh:lb02 back:lb00 weigh:lb03 back:lb01 back:lv00 invert:lv02 exp:lb12 exp:lv11 quant:fa0 quant:sb0 turn:lb13
exp:lb13 back:lv03 weigh:lv02 pool:00 pool:01 exp:lb10 invert:lv11 exp:lb11 gain:00 invert:lb11 back:lv10
gain:01 back:lv02 lay:fa111 back:lv01 quant:lv00 quant:lv03 quant:g0 invert:lb10 cols:03 weigh:lb12 weigh:lb13
weigh:lb11 weigh:lb10 rows:00 rows:03 back:lb11 quant:lv01 back:lb10 lay:fa101 quant:lv02 rows:02 lay:fa100
lay:fa110 quant:fa1 quant:sb1 rows:01 exp:lv12 exp:lv13 cols:00 cols:01 weigh:lv11 pool:10 invert:lv12 gain:10
pool:11 weigh:lv12 gain:11 quant:lv10 quant:g1 back:lv11 quant:lv11 store:00 store:03 invert:lv13 store:01
back:lv12 cols:02 store:02 rows:10 quant:lv12 weigh:lv13 rows:11 cols:10 rows:12 back:lv13 quant:lv13 cols:11
store:10 cols:12 store:11 store:12 rows:13 cols:13 store:13
""".split()

ON_VECTOR = set("cols:10:0 cols:12:0 cols:13:0 lay:fa100:0 lay:fa101:0 lay:fa110:0 rows:11:1 rows:12:0 rows:13:0".split())


def tile_doubleattentiongatherdistributesignedgai_x1_kernel(tc, fa, lb, lv, t, p, r, out_0, out_1, out_2):
    nc = tc.nc
    with ExitStack() as ctx:
        keep = ctx.enter_context(tc.tile_pool(name="keep", bufs=1))
        work = ctx.enter_context(tc.tile_pool(name="work", bufs=1))
        fixed_psum = ctx.enter_context(tc.psum_pool(name="fixed_psum", bufs=1))
        psum = ctx.enter_context(tc.psum_pool(name="psum", bufs=ROTATING_BANKS))
        ctx.enter_context(tc.manual_schedule())

        def kept(name, shape, dtype):
            return keep.tile(shape, dtype, name=name, align_bytes=64)

        def rotating(name, bufs, shape, dtype):
            return work.tile(shape, dtype, name=name, bufs=bufs, align_bytes=64)

        def bank(shape, dtype):
            return psum.tile(shape, dtype, name="bank")

        def copy(step, number, out, in_):
            if "%s:%d" % (step, number) in ON_VECTOR:
                nc.vector.tensor_copy(out=out, in_=in_)
            else:
                nc.scalar.copy(out=out, in_=in_)

        def quantize(codes, scales, in_):
            nc.vector.quantize_mx(out=codes.bitcast(FP8X4), scales=scales, in_=in_)

        def matmul_mx(out, stationary, moving, start, stop):
            nc.tensor.matmul_mx(
                out=out, lhsT=stationary[0].bitcast(FP8X4), lhsT_scale=stationary[1],
                rhs=moving[0].bitcast(FP8X4), rhs_scale=moving[1], start=start, stop=stop,
            )

        r_sb = kept("r_sb", [P, PACK], BF16)
        t_sb = kept("t_sb", [P, PASSES, PACK], BF16)
        p_sb = kept("p_sb", [P, PACK], BF16)
        nc.scalar.dma_start(out=r_sb[:], in_=r.rearrange("(q j) -> q j", j=PACK))
        nc.scalar.dma_start(out=t_sb[:], in_=t.rearrange("(g q j) -> q g j", g=PASSES, j=PACK))
        nc.scalar.dma_start(out=p_sb[:], in_=p.rearrange("(q j) -> q j", j=PACK))

        raw = {}
        for name in LOADS:
            b = int(name[2])
            if name.startswith("lv"):
                first = GROUP * int(name[3])
                raw[name] = kept(name, [P, 2, M], BF16)
                nc.sync.dma_start(out=raw[name][:], in_=lv[b, first : first + GROUP, :].rearrange("(q s) m -> q s m", s=2))
            elif name.startswith("lb"):
                first = HALF * int(name[3])
                raw[name] = kept(name, [P, PASSES, PACK, HALF], BF16)
                for g in range(PASSES):
                    rows = lb[b, P * PACK * g : P * PACK * (g + 1), first : first + HALF]
                    nc.sync.dma_start(out=raw[name][:, g], in_=rows.rearrange("(q j) m -> q j m", j=PACK))
            else:
                raw[name] = kept(name, [P, PASSES, PACK * C], BF16)
                nc.sync.dma_start(out=raw[name][:], in_=fa[b].rearrange("(g q j) c -> q g (j c)", g=PASSES, j=PACK))

        ident32 = kept("ident32", [P, P], F32)
        make_identity(nc, ident32[:])
        zeros = kept("zeros", [P, P], F32)
        nc.vector.memset(zeros[:], 0.0)
        ones = kept("ones", [P, P], BF16)
        nc.scalar.activation(out=ones[:], in_=zeros[:], func=ACT.Exp)
        ident16 = kept("ident16", [P, P], BF16)
        nc.gpsimd.affine_select(
            out=ident16[:], in_=ones[:], compare_op=ALU.is_equal, fill=0.0, base=0, pattern=[[-1, P]], channel_multiplier=1
        )

        r_bank = fixed_psum.tile([P, 2, P], F32, name="r_bank")
        t_bank = bank([P, 2 * PASSES, P], F32)
        for gain_bank, gain_sb in ((r_bank, r_sb[:]), (t_bank, t_sb[:].rearrange("q g j -> q (g j)"))):
            words = gain_sb.bitcast(F32)
            for k in range(words.shape[1]):
                nc.tensor.transpose(gain_bank[:, k, :], words[:, k : k + 1].to_broadcast([P, P]), ident32[:])
        gain_row = {
            "lv": r_bank[:].rearrange("p u q -> p (u q)").bitcast(BF16),
            "lb": t_bank[:].rearrange("p k q -> p (k q)").bitcast(BF16),
        }

        operand = {}
        for b in range(B):
            for name, passes in (("fa%d" % b, PASSES), ("sb%d" % b, PASSES), ("g%d" % b, 1)):
                operand[name] = (
                    kept(name + "_bf16", [P, passes, C * PACK], BF16),
                    kept(name + "_codes", [P, passes, C], U32),
                    kept(name + "_scales", [P, passes, C], U8),
                )
        out_scales = [kept("out_scales%d" % b, [P, N], U8) for b in range(B)]
        words_hbm = out_1[0].rearrange("p m j -> p (m j)").bitcast(I32)
        scales_hbm = out_2[0].bitcast(I32)

        made = {}
        stored = []

        def columns(name, g, first, width):
            bf16, codes, scales = operand[name]
            return codes[:, g, first : first + width], scales[:, g, first : first + width]

        def sums_of(unit):
            owner = unit if unit.startswith("lv") else unit[:3] + str(int(unit[3]) // 2)
            if ("sums", owner) not in made:
                made["sums", owner] = kept("sums_" + owner, [P, 2], F32)
            return owner

        def lay(unit):
            name, g, first = unit[:3], int(unit[3]), HALF * int(unit[4])
            src = raw[name][:, g, :].rearrange("q (j c) -> q j c", j=PACK)[:, :, first : first + HALF]
            dst = operand[name][0][:, g, PACK * first : PACK * (first + HALF)]
            copy("lay:" + unit, 0, dst.rearrange("q (c i j) -> q c j i", i=4, j=PACK), src.rearrange("q j (c i) -> q c j i", i=4))

        def turn(unit):
            a = int(unit[3])
            src = raw[unit[:3] + str(a // 2)]
            turned = bank([P, PASSES * PACK, P], BF16)
            for g in range(PASSES):
                for j in range(PACK):
                    nc.tensor.transpose(turned[:, PACK * g + j, :], src[:, g, j, P * (a % 2) : P * (a % 2 + 1)], ident16[:])
            made["turned", unit] = turned

        def exp(unit):
            of_lb = unit.startswith("lb")
            rows = 1 if of_lb else 2
            width = N // rows
            neg = rotating("neg", NEG_BUFS, [P, rows, width], BF16)
            neg_max = kept("neg_max_" + unit, [P, rows], F32)
            sums = made["sums", sums_of(unit)]
            values = rotating("values", EXP_BUFS, [P, rows, width], F32)
            for s in range(rows):
                src = made["turned", unit][:].rearrange("p k q -> p (k q)") if of_lb else raw[unit][:, s, :]
                nc.vector.tensor_scalar(
                    out=neg[:, s, :], in0=src, scalar1=-1.0, scalar2=None, op0=ALU.mult, op1=ALU.min, accum_out=neg_max[:, s : s + 1]
                )
            for s in range(rows):
                src = neg[:, s, :].rearrange("p (k e q) -> p k q e" if of_lb else "p (q k e) -> p k q e", q=P, e=2)
                column = int(unit[3]) % 2 if of_lb else s
                nc.scalar.activation(
                    out=values[:, s, :].rearrange("p (k q e) -> p k q e", q=P, e=2), in_=src, func=ACT.Exp, scale=-1.0,
                    bias=neg_max[:, s : s + 1], accum_out=sums[:, column : column + 1],
                )
            made["values", unit] = values

        def invert(unit):
            made["inverse", unit] = kept("inverse_" + unit, [P, 2], F32)
            nc.vector.reciprocal(out=made["inverse", unit][:], in_=made["sums", unit][:])

        def weigh(unit):
            values = made["values", unit]
            rows = values.shape[1]
            inverse = made["inverse", sums_of(unit)]
            weighted = rotating("weighted", WEIGHTED_BUFS, list(values.shape), BF16)
            for s in range(rows):
                column = int(unit[3]) % 2 if rows == 1 else s
                nc.vector.scalar_tensor_tensor(
                    out=weighted[:, s, :], in0=values[:, s, :], scalar=inverse[:, column : column + 1],
                    in1=gain_row[unit[:2]], op0=ALU.mult, op1=ALU.mult,
                )
            made["weighted", unit] = weighted

        def back_lb(unit):
            pair = int(unit[3])
            banks = []
            for g in range(PASSES):
                banks.append(bank([P, 2, 2 * P], F32))
                for a in range(2):
                    words = made["weighted", unit[:3] + str(2 * pair + a)][:, 0, :].bitcast(F32)
                    for u in range(2):
                        k = 2 * g + u
                        nc.tensor.transpose(banks[g][:, u, P * a : P * (a + 1)], words[:, P * k : P * (k + 1)], ident32[:])
            share = HALF // PACK
            for g in range(PASSES):
                dst = operand["sb" + unit[2]][0][:, g, :].bitcast(F32).rearrange("q (s i u) -> q s i u", s=PACK, u=2)
                src = banks[g][:].rearrange("q u (i s) -> q s i u", s=PACK)
                copy("back:" + unit, g, dst[:, :, share * pair : share * (pair + 1), :], src)

        def back_lv(unit):
            turned = bank([P, 2, 2, P], F32)
            for s in range(2):
                words = made["weighted", unit][:, s, :].bitcast(F32)
                for u in range(2):
                    nc.tensor.transpose(turned[:, s, u, :], words[:, P * u : P * (u + 1)], ident32[:])
            sv = rotating("sv", SV_BUFS, [P, GROUP * PACK], BF16)
            dst = sv[:].bitcast(F32).rearrange("q (k w) -> q k w", k=P)
            copy("back:" + unit, 0, dst, turned[:].rearrange("q s u k -> q k (s u)"))
            made["sv", unit] = sv

        def back(unit):
            if unit.startswith("lb"):
                back_lb(unit)
            else:
                back_lv(unit)

        def quant(unit):
            if unit.startswith("lv"):
                codes = kept("sv_codes_" + unit, [P, GROUP], U32)
                scales = kept("sv_scales_" + unit, [P, GROUP], U8)
                quantize(codes[:], scales[:], made["sv", unit][:])
                made["sv_mx", unit[2:]] = [(codes[:, P * i : P * (i + 1)], scales[:, P * i : P * (i + 1)]) for i in range(2)]
            else:
                bf16, codes, scales = operand[unit]
                for g in range(bf16.shape[1]):
                    quantize(codes[:, g, :], scales[:, g, :], bf16[:, g, :])

        def pool(unit):
            for chunk in (2 * int(unit[1]), 2 * int(unit[1]) + 1):
                pooled = bank([P, PACK, P], F32)
                for s in range(PACK):
                    for g in range(PASSES):
                        matmul_mx(
                            pooled[:, s, :], columns("sb" + unit[0], g, P * s, P), columns("fa" + unit[0], g, P * chunk, P),
                            start=(g == 0), stop=(g == PASSES - 1),
                        )
                made["pooled", unit[0], chunk] = pooled

        def gain(unit):
            share = P // PACK
            for chunk in (2 * int(unit[1]), 2 * int(unit[1]) + 1):
                dst = operand["g" + unit[0]][0][:, 0, :].rearrange("q (s i j) -> q s i j", s=PACK, j=PACK)
                nc.vector.tensor_tensor(
                    out=dst[:, :, share * chunk : share * (chunk + 1), :],
                    in0=made["pooled", unit[0], chunk][:].rearrange("q j (i s) -> q s i j", s=PACK),
                    in1=p_sb[:].unsqueeze(1).unsqueeze(1).to_broadcast([P, PACK, share, PACK]),
                    op=ALU.mult,
                )

        def rows(unit):
            b, first = int(unit[0]), GROUP * int(unit[1])
            result = rotating("result", ROWS_BUFS, [P, 2, C], F32)
            banks = []
            for i in range(2):
                banks.append(bank([P, C], F32))
                matmul_mx(banks[i][:], made["sv_mx", unit][i], columns("g" + unit[0], 0, 0, C), start=True, stop=True)
            for i in range(2):
                dst = result[:, i, :].rearrange("p (k s) -> p k s", s=PACK)
                copy("rows:" + unit, i, dst, banks[i][:].rearrange("p (s k) -> p k s", s=PACK))
            nc.sync.dma_start(out=out_0[b, first : first + GROUP, :].rearrange("(i p) c -> p i c", i=2), in_=result[:])

        def cols(unit):
            result_bf16 = rotating("result_bf16", COLS_BUFS, [P, 2, P, PACK], BF16)
            banks = []
            for i in range(2):
                banks.append(bank([P, PACK, P], F32))
                for s in range(PACK):
                    matmul_mx(banks[i][:, s, :], columns("g" + unit[0], 0, P * s, P), made["sv_mx", unit][i], start=True, stop=True)
            for i in range(2):
                copy("cols:" + unit, i, result_bf16[:, i], banks[i][:].rearrange("q s k -> q k s"))
            made["result_bf16", unit] = result_bf16

        def store(unit):
            b, first = int(unit[0]), GROUP * int(unit[1])
            codes = rotating("out_codes", CODES_BUFS, [P, GROUP], U32)
            src = made["result_bf16", unit][:].rearrange("q i k s -> q (i k s)")
            quantize(codes[:], out_scales[b][:, first : first + GROUP], src)
            nc.sync.dma_start(out=words_hbm[:, N * b + first : N * b + first + GROUP], in_=codes[:].bitcast(I32))
            stored.append(unit)
            if len([done for done in stored if done[0] == unit[0]]) == GROUPS:
                for quadrant in range(4):
                    queue = nc.scalar if len(stored) == B * GROUPS and quadrant >= 2 else nc.sync
                    queue.dma_start(
                        out=scales_hbm[4 * quadrant : 4 * quadrant + 4, N // 4 * b : N // 4 * (b + 1)],
                        in_=out_scales[b][32 * quadrant : 32 * quadrant + 4, :].bitcast(I32),
                    )

        steps = {
            "lay": lay, "turn": turn, "exp": exp, "invert": invert, "weigh": weigh, "back": back, "quant": quant,
            "pool": pool, "gain": gain, "rows": rows, "cols": cols, "store": store,
        }
        for step in ORDER:
            name, unit = step.split(":")
            steps[name](unit)
